import numpy as np
import ml_dtypes


def mxq(x, axis, fmt="e4m3"):
    dtype, down = {"e4m3": (ml_dtypes.float8_e4m3fn, 7), "e5m2": (ml_dtypes.float8_e5m2, 14)}[fmt]
    v = np.moveaxis(np.asarray(x, np.float32).astype(ml_dtypes.bfloat16).astype(np.float64), axis, -1)
    blocks = v.reshape(v.shape[:-1] + (-1, 32))
    amax = np.abs(blocks).max(-1, keepdims=True)
    byte = np.maximum(np.where(amax > 0, np.frexp(amax)[1] - 1 + 127, 0) - down, 1)
    scale = np.exp2(byte - 127.0)
    codes = (blocks / scale).astype(np.float32).astype(dtype).astype(np.float64)
    return np.moveaxis((codes * scale).reshape(v.shape), -1, axis)


WIDE = False


def mx_kscale(k):
    if not WIDE:
        return np.ones(k)
    levels = np.array([18, -18])
    if k % 512:
        return np.exp2(np.random.permutation(np.resize(levels, k // 32))).repeat(32)
    a = np.empty((k // 512, 16))
    for p in range(k // 512):
        a[p, :8] = np.random.permutation(np.resize(levels, 8))
        for g in range(8):
            far = levels[np.abs(levels - a[p, g]) >= 10]
            a[p, g + 8] = far[np.random.randint(len(far))]
    return np.exp2(a.ravel()).repeat(32)


def f64(x):
    return np.asarray(x).astype(np.float64)


def striped(idx):
    return np.tile(np.asarray(idx).reshape(-1, 16).T, (8, 1)).astype(np.uint16)


def unstriped(offs):
    return offs[:16].T.reshape(-1).astype(np.int64)


B, N, T, D, DV, NQ = 1, 512, 1024, 128, 512, 512


def setup_inputs():
    n = np.random.standard_normal
    idx = np.random.permutation(T)[:B * N]
    s = mx_kscale(DV)[:, None]
    z = mx_kscale(NQ)[:, None]
    p = np.exp(n((B, NQ, N)))
    p = p / p.mean(2, keepdims=True)
    return {
        "doT": (n((B, DV, NQ)) * s / np.sqrt(DV)).astype(np.float32),
        "vT": (n((DV, T)) / s).astype(np.float32),
        "p": (p * z / np.sqrt(NQ)).astype(np.float32),
        "delta": (0.3 * n((B, NQ, 1))).astype(np.float32),
        "qm": (n((B, NQ, D)) / z).astype(np.float32),
        "offs": striped(idx),
    }


def reference(doT, vT, p, delta, qm, offs):
    idx = unstriped(offs)
    pick = lambda x: x[:, idx].reshape(x.shape[0], B, N).transpose(1, 0, 2)
    dp = mxq(f64(doT), 1, "e5m2").transpose(0, 2, 1) @ mxq(pick(f64(vT)), 1, "e4m3")
    ds = f64(p) * (dp - f64(delta))
    dk = mxq(f64(qm), 1, "e4m3").transpose(0, 2, 1) @ mxq(ds, 1, "e5m2")
    out = np.zeros((D, T))
    out[:, idx] = dk.transpose(1, 0, 2).reshape(D, B * N)
    return out

@@ -1,0 +1,190 @@
+from contextlib import ExitStack
+
+import concourse.mybir as mybir
+
+FLOPS = 335544320
+
+F32 = mybir.dt.float32
+BF16 = mybir.dt.bfloat16
+U32 = mybir.dt.uint32
+U16 = mybir.dt.uint16
+U8 = mybir.dt.uint8
+E4M3X4 = mybir.dt.float8_e4m3fn_x4
+E5M2X4 = mybir.dt.float8_e5m2_x4
+ACT = mybir.ActivationFunctionType
+ALU = mybir.AluOpType
+
+P = 128
+J = 4
+E = 512
+Q = 512
+N = 512
+T = 1024
+D = 128
+H = 2
+NH = N // H
+TH = T // 2
+QH = Q // 2
+
+
+def tile_attend_bwd_kernel(tc, doT, vT, p, delta, qm, offs, out):
+    nc = tc.nc
+    with ExitStack() as ctx:
+        keep = ctx.enter_context(tc.tile_pool(name="keep", bufs=1))
+        psum = ctx.enter_context(tc.psum_pool(name="psum", bufs=1))
+
+        offsets = keep.tile([P, N // 16], U16, name="offsets")
+
+        v_rows = vT.rearrange("(p j) t -> p j t", j=J)
+        v_raw = {}
+        for g in range(2):
+            for h in range(2):
+                v_raw[g, h] = keep.tile([P, 2, TH], F32, name=f"v_raw{g}{h}")
+        nc.sync.dma_start(out=v_raw[0, 0][:], in_=v_rows[:, 0:2, 0:TH])
+        nc.sync.dma_start(offsets[:], offs)
+        nc.sync.dma_start(out=v_raw[0, 1][:], in_=v_rows[:, 0:2, TH:T])
+        for h in range(2):
+            nc.sync.dma_start(out=v_raw[1, h][:], in_=v_rows[:, 2:4, h * TH : (h + 1) * TH])
+
+        do_rows = doT[0].rearrange("(p j) q -> p j q", j=J)
+        do_raw = []
+        for h in range(2):
+            t = keep.tile([P, J, QH], F32, name=f"do_raw{h}")
+            nc.sync.dma_start(out=t[:], in_=do_rows[:, :, h * QH : (h + 1) * QH])
+            do_raw.append(t)
+
+        qm_raw = keep.tile([P, J, D], F32, name="qm_raw")
+        nc.sync.dma_start(out=qm_raw[:], in_=qm[0].rearrange("(p j) d -> p j d", j=J))
+
+        p_rows = p[0].rearrange("(p j) s -> p j s", j=J)
+        p_raw = []
+        for h in range(H):
+            t = keep.tile([P, J, NH], F32, name=f"p_raw{h}")
+            nc.sync.dma_start(out=t[:], in_=p_rows[:, :, h * NH : (h + 1) * NH])
+            p_raw.append(t)
+
+        delta_col = keep.tile([P, J], F32, name="delta_col")
+        nc.scalar.dma_start(out=delta_col[:], in_=delta[0].rearrange("(p j) o -> p (j o)", j=J))
+        minus_delta = keep.tile([P, J], F32, name="minus_delta")
+        nc.gpsimd.tensor_scalar(minus_delta[:], delta_col[:], -1.0, None, ALU.mult)
+
+        warm = keep.tile([P, 1], F32, name="warm")
+        warm_out = keep.tile([P, 1], F32, name="warm_out")
+        nc.gpsimd.memset(warm[:], 0.0)
+        nc.scalar.activation(warm_out[:], warm[:], ACT.Identity)
+        window = keep.tile([P, T], F32, name="window")
+        nc.gpsimd.memset(window[:], 0.0)
+        ds_codes = []
+        ds_scales = []
+        for h in range(H):
+            c = keep.tile([P, N], U32, name=f"ds_codes{h}", align_bytes=64)
+            s = keep.tile([P, N], U8, name=f"ds_scales{h}", align_bytes=64)
+            o = (1 - h) * NH
+            nc.gpsimd.memset(c[:, o : o + NH], 0)
+            nc.gpsimd.memset(s[:, o : o + NH], 0)
+            ds_codes.append(c)
+            ds_scales.append(s)
+
+        v_win = []
+        for g in range(2):
+            w = keep.tile([P, 2 * T], BF16, name=f"v_win{g}", align_bytes=64)
+            v_win.append(w)
+        v_cols = keep.tile([P, J * N], BF16, name="v_cols", align_bytes=64)
+        v_words = v_cols[:].bitcast(U32).rearrange("p (s g) -> p g s", g=2)
+
+        def pack(g, h, on_scalar):
+            dst = v_win[g][:, h * 2 * TH : (h + 1) * 2 * TH].rearrange("p (c i j) -> p c j i", i=4, j=2)
+            src = v_raw[g, h][:].rearrange("p j (c i) -> p c j i", i=4)
+            if on_scalar:
+                nc.scalar.activation(dst, src, ACT.Copy)
+            else:
+                nc.vector.tensor_copy(dst, src)
+
+        pack(0, 0, False)
+        pack(0, 1, False)
+        nc.vector.tensor_copy(v_words[:, 0, :], v_win[0][:].bitcast(U32).indirect(offsets[:]))
+        pack(1, 0, True)
+        pack(1, 1, False)
+        nc.vector.tensor_copy(v_words[:, 1, :], v_win[1][:].bitcast(U32).indirect(offsets[:]))
+
+        do_cols = keep.tile([P, J * Q], BF16, name="do_cols", align_bytes=64)
+        do_view = do_cols[:].rearrange("p (t m j) -> p m j t", t=J, j=J)
+        MH = QH // J
+        for h, m0, m1 in ((0, 0, MH), (1, 0, MH // 2), (1, MH // 2, MH)):
+            dst = do_view[:, h * MH + m0 : h * MH + m1, :, :]
+            src = do_raw[h][:, :, m0 * J : m1 * J].rearrange("p j (m t) -> p m j t", t=J)
+            if m0 == 0:
+                nc.scalar.activation(dst, src, ACT.Copy)
+            else:
+                nc.vector.tensor_copy(dst, src)
+        v_codes = keep.tile([P, N], U32, name="v_codes", align_bytes=64)
+        v_scales = keep.tile([P, N], U8, name="v_scales", align_bytes=64)
+        nc.vector.quantize_mx(out=v_codes[:].bitcast(E4M3X4), scales=v_scales[:], in_=v_cols[:])
+
+        qm_cols = keep.tile([P, J * D], BF16, name="qm_cols", align_bytes=64)
+        nc.scalar.activation(
+            qm_cols[:].rearrange("p (c i j) -> p c j i", i=4, j=J),
+            qm_raw[:].rearrange("p j (c i) -> p c j i", i=4),
+            ACT.Copy,
+        )
+
+        do_codes = keep.tile([P, Q], U32, name="do_codes", align_bytes=64)
+        do_scales = keep.tile([P, Q], U8, name="do_scales", align_bytes=64)
+        dp = []
+        for t in range(J):
+            cols = slice(t * P, (t + 1) * P)
+            nc.vector.quantize_mx(
+                out=do_codes[:, cols].bitcast(E5M2X4),
+                scales=do_scales[:, cols],
+                in_=do_cols[:, t * P * J : (t + 1) * P * J],
+            )
+            bank = psum.tile([P, N], F32, name=f"dp{t}")
+            nc.tensor.matmul_mx(
+                out=bank[:],
+                lhsT=do_codes[:, cols].bitcast(E5M2X4),
+                lhsT_scale=do_scales[:, cols],
+                rhs=v_codes[:].bitcast(E4M3X4),
+                rhs_scale=v_scales[:],
+                start=True,
+                stop=True,
+            )
+            dp.append(bank)
+
+        qm_codes = keep.tile([P, D], U32, name="qm_codes", align_bytes=64)
+        qm_scales = keep.tile([P, D], U8, name="qm_scales", align_bytes=64)
+        nc.vector.quantize_mx(out=qm_codes[:].bitcast(E4M3X4), scales=qm_scales[:], in_=qm_cols[:])
+
+        for h in range(H):
+            slots = slice(h * NH, (h + 1) * NH)
+            x = keep.tile([P, J, NH], F32, name=f"x{h}")
+            for t in range(J):
+                nc.scalar.activation(x[:, t, :], dp[t][:, slots], ACT.Identity, bias=minus_delta[:, t : t + 1])
+            ds_cols = keep.tile([P, J * NH], BF16, name=f"ds_cols{h}", align_bytes=64)
+            nc.vector.tensor_tensor(
+                ds_cols[:].rearrange("p (c i j) -> p c j i", i=4, j=J),
+                x[:].rearrange("p j (c i) -> p c j i", i=4),
+                p_raw[h][:].rearrange("p j (c i) -> p c j i", i=4),
+                ALU.mult,
+            )
+            nc.vector.quantize_mx(
+                out=ds_codes[h][:, slots].bitcast(E5M2X4),
+                scales=ds_scales[h][:, slots],
+                in_=ds_cols[:],
+            )
+
+        for h in range(H):
+            slots = slice(h * NH, (h + 1) * NH)
+            dk = psum.tile([P, N], F32, name=f"dk{h}")
+            nc.tensor.matmul_mx(
+                out=dk[:],
+                lhsT=qm_codes[:].bitcast(E4M3X4),
+                lhsT_scale=qm_scales[:],
+                rhs=ds_codes[h][:].bitcast(E5M2X4),
+                rhs_scale=ds_scales[h][:],
+                start=True,
+                stop=True,
+            )
+            dk_cols = keep.tile([P, NH], F32, name=f"dk_cols{h}")
+            nc.scalar.activation(dk_cols[:], dk[:, slots], ACT.Copy)
+            nc.vector.tensor_copy(window[:].indirect(offsets[:, h * (NH // 16) : (h + 1) * (NH // 16)]), dk_cols[:])
+        nc.sync.dma_start(out=out, in_=window[:])

@@ -23,7 +23,8 @@ T = 1024
 D = 128
 H = 2
 NH = N // H
-TH = T // 2
+NA = 128
+TV = 640
 QH = Q // 2
 
 
@@ -36,15 +37,12 @@ def tile_attend_bwd_kernel(tc, doT, vT, p, delta, qm, offs, out):
         offsets = keep.tile([P, N // 16], U16, name="offsets")
 
         v_rows = vT.rearrange("(p j) t -> p j t", j=J)
-        v_raw = {}
+        v_raw = []
         for g in range(2):
-            for h in range(2):
-                v_raw[g, h] = keep.tile([P, 2, TH], F32, name=f"v_raw{g}{h}")
-        nc.sync.dma_start(out=v_raw[0, 0][:], in_=v_rows[:, 0:2, 0:TH])
+            v_raw.append(keep.tile([P, 2, T], F32, name=f"v_raw{g}"))
+        nc.sync.dma_start(out=v_raw[0][:], in_=v_rows[:, 0:2, :])
         nc.sync.dma_start(offsets[:], offs)
-        nc.sync.dma_start(out=v_raw[0, 1][:], in_=v_rows[:, 0:2, TH:T])
-        for h in range(2):
-            nc.sync.dma_start(out=v_raw[1, h][:], in_=v_rows[:, 2:4, h * TH : (h + 1) * TH])
+        nc.sync.dma_start(out=v_raw[1][:], in_=v_rows[:, 2:4, :])
 
         do_rows = doT[0].rearrange("(p j) q -> p j q", j=J)
         do_raw = []
@@ -57,11 +55,11 @@ def tile_attend_bwd_kernel(tc, doT, vT, p, delta, qm, offs, out):
         nc.sync.dma_start(out=qm_raw[:], in_=qm[0].rearrange("(p j) d -> p j d", j=J))
 
         p_rows = p[0].rearrange("(p j) s -> p j s", j=J)
-        p_raw = []
-        for h in range(H):
+        p_raw = {}
+        for h in (1, 0):
             t = keep.tile([P, J, NH], F32, name=f"p_raw{h}")
             nc.sync.dma_start(out=t[:], in_=p_rows[:, :, h * NH : (h + 1) * NH])
-            p_raw.append(t)
+            p_raw[h] = t
 
         delta_col = keep.tile([P, J], F32, name="delta_col")
         nc.scalar.dma_start(out=delta_col[:], in_=delta[0].rearrange("(p j) o -> p (j o)", j=J))
@@ -76,12 +74,12 @@ def tile_attend_bwd_kernel(tc, doT, vT, p, delta, qm, offs, out):
         nc.gpsimd.memset(window[:], 0.0)
         ds_codes = []
         ds_scales = []
-        for h in range(H):
+        for h in range(2):
             c = keep.tile([P, N], U32, name=f"ds_codes{h}", align_bytes=64)
             s = keep.tile([P, N], U8, name=f"ds_scales{h}", align_bytes=64)
-            o = (1 - h) * NH
-            nc.gpsimd.memset(c[:, o : o + NH], 0)
-            nc.gpsimd.memset(s[:, o : o + NH], 0)
+            fill = slice(NA, N) if h == 0 else slice(0, NA)
+            nc.gpsimd.memset(c[:, fill], 0)
+            nc.gpsimd.memset(s[:, fill].bitcast(U32), 0)
             ds_codes.append(c)
             ds_scales.append(s)
 
@@ -92,19 +90,18 @@ def tile_attend_bwd_kernel(tc, doT, vT, p, delta, qm, offs, out):
         v_cols = keep.tile([P, J * N], BF16, name="v_cols", align_bytes=64)
         v_words = v_cols[:].bitcast(U32).rearrange("p (s g) -> p g s", g=2)
 
-        def pack(g, h, on_scalar):
-            dst = v_win[g][:, h * 2 * TH : (h + 1) * 2 * TH].rearrange("p (c i j) -> p c j i", i=4, j=2)
-            src = v_raw[g, h][:].rearrange("p j (c i) -> p c j i", i=4)
-            if on_scalar:
-                nc.scalar.activation(dst, src, ACT.Copy)
-            else:
-                nc.vector.tensor_copy(dst, src)
+        def pack(g):
+            for t0, t1, on_scalar in ((0, TV, False), (TV, T, True)):
+                dst = v_win[g][:, 2 * t0 : 2 * t1].rearrange("p (c i j) -> p c j i", i=4, j=2)
+                src = v_raw[g][:, :, t0:t1].rearrange("p j (c i) -> p c j i", i=4)
+                if on_scalar:
+                    nc.scalar.activation(dst, src, ACT.Copy)
+                else:
+                    nc.vector.tensor_copy(dst, src)
 
-        pack(0, 0, False)
-        pack(0, 1, False)
+        pack(0)
         nc.vector.tensor_copy(v_words[:, 0, :], v_win[0][:].bitcast(U32).indirect(offsets[:]))
-        pack(1, 0, True)
-        pack(1, 1, False)
+        pack(1)
         nc.vector.tensor_copy(v_words[:, 1, :], v_win[1][:].bitcast(U32).indirect(offsets[:]))
 
         do_cols = keep.tile([P, J * Q], BF16, name="do_cols", align_bytes=64)
@@ -120,13 +117,6 @@ def tile_attend_bwd_kernel(tc, doT, vT, p, delta, qm, offs, out):
         v_codes = keep.tile([P, N], U32, name="v_codes", align_bytes=64)
         v_scales = keep.tile([P, N], U8, name="v_scales", align_bytes=64)
         nc.vector.quantize_mx(out=v_codes[:].bitcast(E4M3X4), scales=v_scales[:], in_=v_cols[:])
-
-        qm_cols = keep.tile([P, J * D], BF16, name="qm_cols", align_bytes=64)
-        nc.scalar.activation(
-            qm_cols[:].rearrange("p (c i j) -> p c j i", i=4, j=J),
-            qm_raw[:].rearrange("p j (c i) -> p c j i", i=4),
-            ACT.Copy,
-        )
 
         do_codes = keep.tile([P, Q], U32, name="do_codes", align_bytes=64)
         do_scales = keep.tile([P, Q], U8, name="do_scales", align_bytes=64)
@@ -150,30 +140,49 @@ def tile_attend_bwd_kernel(tc, doT, vT, p, delta, qm, offs, out):
             )
             dp.append(bank)
 
+        qm_cols = keep.tile([P, J * D], BF16, name="qm_cols", align_bytes=64)
+        nc.gpsimd.tensor_scalar(
+            qm_cols[:].rearrange("p (c i j) -> p c j i", i=4, j=J),
+            qm_raw[:].rearrange("p j (c i) -> p c j i", i=4),
+            1.0,
+            0.0,
+            ALU.mult,
+            ALU.add,
+        )
         qm_codes = keep.tile([P, D], U32, name="qm_codes", align_bytes=64)
         qm_scales = keep.tile([P, D], U8, name="qm_scales", align_bytes=64)
         nc.vector.quantize_mx(out=qm_codes[:].bitcast(E4M3X4), scales=qm_scales[:], in_=qm_cols[:])
 
-        for h in range(H):
-            slots = slice(h * NH, (h + 1) * NH)
-            x = keep.tile([P, J, NH], F32, name=f"x{h}")
-            for t in range(J):
-                nc.scalar.activation(x[:, t, :], dp[t][:, slots], ACT.Identity, bias=minus_delta[:, t : t + 1])
-            ds_cols = keep.tile([P, J * NH], BF16, name=f"ds_cols{h}", align_bytes=64)
+        x = keep.tile([P, J, NH], F32, name="x")
+        ds_rows = keep.tile([P, J, NH], BF16, name="ds_rows")
+        for t in range(J):
+            nc.scalar.activation(x[:, t, :], dp[t][:, 0:NH], ACT.Identity, bias=minus_delta[:, t : t + 1])
+            nc.vector.scalar_tensor_tensor(
+                ds_rows[:, t, :], dp[t][:, NH:N], delta_col[:, t : t + 1], p_raw[1][:, t, :], ALU.subtract, ALU.mult
+            )
+        ds_tail = keep.tile([P, J * NH], BF16, name="ds_tail", align_bytes=64)
+        nc.scalar.copy(
+            ds_tail[:].rearrange("p (c i j) -> p c j i", i=4, j=J),
+            ds_rows[:].rearrange("p j (c i) -> p c j i", i=4),
+        )
+        ds_head = []
+        for a in range(2):
+            cols = slice(a * NA, (a + 1) * NA)
+            d = keep.tile([P, J * NA], BF16, name=f"ds_head{a}", align_bytes=64)
             nc.vector.tensor_tensor(
-                ds_cols[:].rearrange("p (c i j) -> p c j i", i=4, j=J),
-                x[:].rearrange("p j (c i) -> p c j i", i=4),
-                p_raw[h][:].rearrange("p j (c i) -> p c j i", i=4),
+                d[:].rearrange("p (c i j) -> p c j i", i=4, j=J),
+                x[:, :, cols].rearrange("p j (c i) -> p c j i", i=4),
+                p_raw[0][:, :, cols].rearrange("p j (c i) -> p c j i", i=4),
                 ALU.mult,
             )
-            nc.vector.quantize_mx(
-                out=ds_codes[h][:, slots].bitcast(E5M2X4),
-                scales=ds_scales[h][:, slots],
-                in_=ds_cols[:],
-            )
+            ds_head.append(d)
 
-        for h in range(H):
-            slots = slice(h * NH, (h + 1) * NH)
+        def quantise_ds(h, cols, src):
+            nc.vector.quantize_mx(out=ds_codes[h][:, cols].bitcast(E5M2X4), scales=ds_scales[h][:, cols], in_=src[:])
+
+        dk_cols = []
+
+        def keys_gradient(h, cols):
             dk = psum.tile([P, N], F32, name=f"dk{h}")
             nc.tensor.matmul_mx(
                 out=dk[:],
@@ -184,7 +193,16 @@ def tile_attend_bwd_kernel(tc, doT, vT, p, delta, qm, offs, out):
                 start=True,
                 stop=True,
             )
-            dk_cols = keep.tile([P, NH], F32, name=f"dk_cols{h}")
-            nc.scalar.activation(dk_cols[:], dk[:, slots], ACT.Copy)
-            nc.vector.tensor_copy(window[:].indirect(offsets[:, h * (NH // 16) : (h + 1) * (NH // 16)]), dk_cols[:])
+            for c0, c1 in cols:
+                d = keep.tile([P, c1 - c0], F32, name=f"dk_cols{c0}")
+                nc.scalar.activation(d[:], dk[:, c0:c1], ACT.Copy)
+                dk_cols.append((c0, c1, d))
+
+        quantise_ds(0, slice(0, NA), ds_head[0])
+        keys_gradient(0, ((0, NA),))
+        quantise_ds(1, slice(NA, NH), ds_head[1])
+        quantise_ds(1, slice(NH, N), ds_tail)
+        keys_gradient(1, ((NA, N),))
+        for c0, c1, d in dk_cols:
+            nc.vector.tensor_copy(window[:].indirect(offsets[:, c0 // 16 : c1 // 16]), d[:])
         nc.sync.dma_start(out=out, in_=window[:])

@@ -1,6 +1,7 @@
 from contextlib import ExitStack
 
 import concourse.mybir as mybir
+from concourse.masks import make_identity
 
 FLOPS = 335544320
 
@@ -24,7 +25,7 @@ D = 128
 H = 2
 NH = N // H
 NA = 128
-TV = 640
+NV = 320
 QH = Q // 2
 
 
@@ -38,11 +39,12 @@ def tile_attend_bwd_kernel(tc, doT, vT, p, delta, qm, offs, out):
 
         v_rows = vT.rearrange("(p j) t -> p j t", j=J)
         v_raw = []
-        for g in range(2):
-            v_raw.append(keep.tile([P, 2, T], F32, name=f"v_raw{g}"))
-        nc.sync.dma_start(out=v_raw[0][:], in_=v_rows[:, 0:2, :])
-        nc.sync.dma_start(offsets[:], offs)
-        nc.sync.dma_start(out=v_raw[1][:], in_=v_rows[:, 2:4, :])
+        for j in range(J):
+            t = keep.tile([P, T], F32, name=f"v_raw{j}")
+            nc.sync.dma_start(out=t[:], in_=v_rows[:, j, :])
+            v_raw.append(t)
+            if j == 0:
+                nc.sync.dma_start(offsets[:], offs)
 
         do_rows = doT[0].rearrange("(p j) q -> p j q", j=J)
         do_raw = []
@@ -83,30 +85,46 @@ def tile_attend_bwd_kernel(tc, doT, vT, p, delta, qm, offs, out):
             ds_codes.append(c)
             ds_scales.append(s)
 
-        v_win = []
-        for g in range(2):
-            w = keep.tile([P, 2 * T], BF16, name=f"v_win{g}", align_bytes=64)
-            v_win.append(w)
+        identity = keep.tile([P, P], F32, name="identity")
+        make_identity(nc, identity[:])
+        spare = []
+        for b in range(2):
+            spare.append(psum.tile([P, 4, P], F32, name=f"spare{b}"))
+        turns = [0]
+
+        def keep_warm(src):
+            b = turns[0] % 8
+            turns[0] += 1
+            nc.tensor.transpose(spare[b // 4][:, b % 4, :], src, identity[:])
+
+        v_got = keep.tile([P, J, N], F32, name="v_got")
         v_cols = keep.tile([P, J * N], BF16, name="v_cols", align_bytes=64)
-        v_words = v_cols[:].bitcast(U32).rearrange("p (s g) -> p g s", g=2)
 
-        def pack(g):
-            for t0, t1, on_scalar in ((0, TV, False), (TV, T, True)):
-                dst = v_win[g][:, 2 * t0 : 2 * t1].rearrange("p (c i j) -> p c j i", i=4, j=2)
-                src = v_raw[g][:, :, t0:t1].rearrange("p j (c i) -> p c j i", i=4)
-                if on_scalar:
-                    nc.scalar.activation(dst, src, ACT.Copy)
-                else:
-                    nc.vector.tensor_copy(dst, src)
+        def interleave_v(engine_copy, pair, s0, s1):
+            js = slice(2 * pair, 2 * pair + 2)
+            engine_copy(
+                v_cols[:, J * s0 : J * s1].rearrange("p (c i j) -> p c j i", i=4, j=J)[:, :, js, :],
+                v_got[:, js, s0:s1].rearrange("p j (c i) -> p c j i", i=4),
+            )
 
-        pack(0)
-        nc.vector.tensor_copy(v_words[:, 0, :], v_win[0][:].bitcast(U32).indirect(offsets[:]))
-        pack(1)
-        nc.vector.tensor_copy(v_words[:, 1, :], v_win[1][:].bitcast(U32).indirect(offsets[:]))
+        for j in range(J):
+            nc.vector.tensor_copy(v_got[:, j, :], v_raw[j][:].indirect(offsets[:]))
+            if j == 1:
+                interleave_v(nc.scalar.copy, 0, 0, N)
+        for b in range(10):
+            keep_warm(v_raw[3][:, b % 8 * P : (b % 8 + 1) * P])
+        for h, n in ((0, 8), (1, 6)):
+            for b in range(n):
+                keep_warm(do_raw[h][:, b // 2, b % 2 * P : (b % 2 + 1) * P])
+        interleave_v(nc.vector.tensor_copy, 1, 0, NV)
+        interleave_v(nc.scalar.copy, 1, NV, N)
 
         do_cols = keep.tile([P, J * Q], BF16, name="do_cols", align_bytes=64)
         do_view = do_cols[:].rearrange("p (t m j) -> p m j t", t=J, j=J)
         MH = QH // J
+        v_codes = keep.tile([P, N], U32, name="v_codes", align_bytes=64)
+        v_scales = keep.tile([P, N], U8, name="v_scales", align_bytes=64)
+        nc.vector.quantize_mx(out=v_codes[:].bitcast(E4M3X4), scales=v_scales[:], in_=v_cols[:])
         for h, m0, m1 in ((0, 0, MH), (1, 0, MH // 2), (1, MH // 2, MH)):
             dst = do_view[:, h * MH + m0 : h * MH + m1, :, :]
             src = do_raw[h][:, :, m0 * J : m1 * J].rearrange("p j (m t) -> p m j t", t=J)
@@ -114,9 +132,6 @@ def tile_attend_bwd_kernel(tc, doT, vT, p, delta, qm, offs, out):
                 nc.scalar.activation(dst, src, ACT.Copy)
             else:
                 nc.vector.tensor_copy(dst, src)
-        v_codes = keep.tile([P, N], U32, name="v_codes", align_bytes=64)
-        v_scales = keep.tile([P, N], U8, name="v_scales", align_bytes=64)
-        nc.vector.quantize_mx(out=v_codes[:].bitcast(E4M3X4), scales=v_scales[:], in_=v_cols[:])
 
         do_codes = keep.tile([P, Q], U32, name="do_codes", align_bytes=64)
         do_scales = keep.tile([P, Q], U8, name="do_scales", align_bytes=64)
@@ -141,13 +156,10 @@ def tile_attend_bwd_kernel(tc, doT, vT, p, delta, qm, offs, out):
             dp.append(bank)
 
         qm_cols = keep.tile([P, J * D], BF16, name="qm_cols", align_bytes=64)
-        nc.gpsimd.tensor_scalar(
+        nc.scalar.activation(
             qm_cols[:].rearrange("p (c i j) -> p c j i", i=4, j=J),
             qm_raw[:].rearrange("p j (c i) -> p c j i", i=4),
-            1.0,
-            0.0,
-            ALU.mult,
-            ALU.add,
+            ACT.Copy,
         )
         qm_codes = keep.tile([P, D], U32, name="qm_codes", align_bytes=64)
         qm_scales = keep.tile([P, D], U8, name="qm_scales", align_bytes=64)
@@ -160,25 +172,27 @@ def tile_attend_bwd_kernel(tc, doT, vT, p, delta, qm, offs, out):
             nc.vector.scalar_tensor_tensor(
                 ds_rows[:, t, :], dp[t][:, NH:N], delta_col[:, t : t + 1], p_raw[1][:, t, :], ALU.subtract, ALU.mult
             )
+        for t in range(J):
+            for b in range(NH // P):
+                keep_warm(x[:, t, b * P : (b + 1) * P])
+        for t in range(J):
+            for b in range(NH // P):
+                keep_warm(p_raw[0][:, t, b * P : (b + 1) * P])
         ds_tail = keep.tile([P, J * NH], BF16, name="ds_tail", align_bytes=64)
         nc.scalar.copy(
             ds_tail[:].rearrange("p (c i j) -> p c j i", i=4, j=J),
             ds_rows[:].rearrange("p j (c i) -> p c j i", i=4),
         )
-        ds_head = []
-        for a in range(2):
-            cols = slice(a * NA, (a + 1) * NA)
-            d = keep.tile([P, J * NA], BF16, name=f"ds_head{a}", align_bytes=64)
-            nc.vector.tensor_tensor(
-                d[:].rearrange("p (c i j) -> p c j i", i=4, j=J),
-                x[:, :, cols].rearrange("p j (c i) -> p c j i", i=4),
-                p_raw[0][:, :, cols].rearrange("p j (c i) -> p c j i", i=4),
-                ALU.mult,
-            )
-            ds_head.append(d)
+        ds_head = keep.tile([P, J * NH], BF16, name="ds_head", align_bytes=64)
+        nc.vector.tensor_tensor(
+            ds_head[:].rearrange("p (c i j) -> p c j i", i=4, j=J),
+            x[:].rearrange("p j (c i) -> p c j i", i=4),
+            p_raw[0][:].rearrange("p j (c i) -> p c j i", i=4),
+            ALU.mult,
+        )
 
         def quantise_ds(h, cols, src):
-            nc.vector.quantize_mx(out=ds_codes[h][:, cols].bitcast(E5M2X4), scales=ds_scales[h][:, cols], in_=src[:])
+            nc.vector.quantize_mx(out=ds_codes[h][:, cols].bitcast(E5M2X4), scales=ds_scales[h][:, cols], in_=src)
 
         dk_cols = []
 
@@ -198,10 +212,10 @@ def tile_attend_bwd_kernel(tc, doT, vT, p, delta, qm, offs, out):
                 nc.scalar.activation(d[:], dk[:, c0:c1], ACT.Copy)
                 dk_cols.append((c0, c1, d))
 
-        quantise_ds(0, slice(0, NA), ds_head[0])
+        quantise_ds(0, slice(0, NA), ds_head[:, 0 : J * NA])
         keys_gradient(0, ((0, NA),))
-        quantise_ds(1, slice(NA, NH), ds_head[1])
-        quantise_ds(1, slice(NH, N), ds_tail)
+        quantise_ds(1, slice(NA, NH), ds_head[:, J * NA : J * NH])
+        quantise_ds(1, slice(NH, N), ds_tail[:])
         keys_gradient(1, ((NA, N),))
         for c0, c1, d in dk_cols:
             nc.vector.tensor_copy(window[:].indirect(offsets[:, c0 // 16 : c1 // 16]), d[:])

@@ -53,15 +53,15 @@ def tile_attend_bwd_kernel(tc, doT, vT, p, delta, qm, offs, out):
             nc.sync.dma_start(out=t[:], in_=do_rows[:, :, h * QH : (h + 1) * QH])
             do_raw.append(t)
 
-        qm_raw = keep.tile([P, J, D], F32, name="qm_raw")
-        nc.sync.dma_start(out=qm_raw[:], in_=qm[0].rearrange("(p j) d -> p j d", j=J))
-
         p_rows = p[0].rearrange("(p j) s -> p j s", j=J)
         p_raw = {}
         for h in (1, 0):
             t = keep.tile([P, J, NH], F32, name=f"p_raw{h}")
             nc.sync.dma_start(out=t[:], in_=p_rows[:, :, h * NH : (h + 1) * NH])
             p_raw[h] = t
+            if h == 1:
+                qm_raw = keep.tile([P, J, D], F32, name="qm_raw")
+                nc.sync.dma_start(out=qm_raw[:], in_=qm[0].rearrange("(p j) d -> p j d", j=J))
 
         delta_col = keep.tile([P, J], F32, name="delta_col")
         nc.scalar.dma_start(out=delta_col[:], in_=delta[0].rearrange("(p j) o -> p (j o)", j=J))
@@ -156,14 +156,16 @@ def tile_attend_bwd_kernel(tc, doT, vT, p, delta, qm, offs, out):
             dp.append(bank)
 
         qm_cols = keep.tile([P, J * D], BF16, name="qm_cols", align_bytes=64)
-        nc.scalar.activation(
+        nc.gpsimd.tensor_scalar(
             qm_cols[:].rearrange("p (c i j) -> p c j i", i=4, j=J),
             qm_raw[:].rearrange("p j (c i) -> p c j i", i=4),
-            ACT.Copy,
+            1.0,
+            0.0,
+            ALU.mult,
+            ALU.add,
         )
         qm_codes = keep.tile([P, D], U32, name="qm_codes", align_bytes=64)
         qm_scales = keep.tile([P, D], U8, name="qm_scales", align_bytes=64)
-        nc.vector.quantize_mx(out=qm_codes[:].bitcast(E4M3X4), scales=qm_scales[:], in_=qm_cols[:])
 
         x = keep.tile([P, J, NH], F32, name="x")
         ds_rows = keep.tile([P, J, NH], BF16, name="ds_rows")
@@ -183,13 +185,18 @@ def tile_attend_bwd_kernel(tc, doT, vT, p, delta, qm, offs, out):
             ds_tail[:].rearrange("p (c i j) -> p c j i", i=4, j=J),
             ds_rows[:].rearrange("p j (c i) -> p c j i", i=4),
         )
-        ds_head = keep.tile([P, J * NH], BF16, name="ds_head", align_bytes=64)
-        nc.vector.tensor_tensor(
-            ds_head[:].rearrange("p (c i j) -> p c j i", i=4, j=J),
-            x[:].rearrange("p j (c i) -> p c j i", i=4),
-            p_raw[0][:].rearrange("p j (c i) -> p c j i", i=4),
-            ALU.mult,
-        )
+        nc.vector.quantize_mx(out=qm_codes[:].bitcast(E4M3X4), scales=qm_scales[:], in_=qm_cols[:])
+        ds_head = []
+        for a in range(2):
+            cols = slice(a * NA, (a + 1) * NA)
+            d = keep.tile([P, J * NA], BF16, name=f"ds_head{a}", align_bytes=64)
+            nc.vector.tensor_tensor(
+                d[:].rearrange("p (c i j) -> p c j i", i=4, j=J),
+                x[:, :, cols].rearrange("p j (c i) -> p c j i", i=4),
+                p_raw[0][:, :, cols].rearrange("p j (c i) -> p c j i", i=4),
+                ALU.mult,
+            )
+            ds_head.append(d)
 
         def quantise_ds(h, cols, src):
             nc.vector.quantize_mx(out=ds_codes[h][:, cols].bitcast(E5M2X4), scales=ds_scales[h][:, cols], in_=src)
@@ -212,9 +219,9 @@ def tile_attend_bwd_kernel(tc, doT, vT, p, delta, qm, offs, out):
                 nc.scalar.activation(d[:], dk[:, c0:c1], ACT.Copy)
                 dk_cols.append((c0, c1, d))
 
-        quantise_ds(0, slice(0, NA), ds_head[:, 0 : J * NA])
+        quantise_ds(0, slice(0, NA), ds_head[0][:])
         keys_gradient(0, ((0, NA),))
-        quantise_ds(1, slice(NA, NH), ds_head[:, J * NA : J * NH])
+        quantise_ds(1, slice(NA, NH), ds_head[1][:])
         quantise_ds(1, slice(NH, N), ds_tail[:])
         keys_gradient(1, ((NA, N),))
         for c0, c1, d in dk_cols:

from contextlib import ExitStack

import concourse.mybir as mybir
from concourse.masks import make_identity

FLOPS = 335544320

F32 = mybir.dt.float32
BF16 = mybir.dt.bfloat16
U32 = mybir.dt.uint32
U16 = mybir.dt.uint16
U8 = mybir.dt.uint8
E4M3X4 = mybir.dt.float8_e4m3fn_x4
E5M2X4 = mybir.dt.float8_e5m2_x4
ACT = mybir.ActivationFunctionType
ALU = mybir.AluOpType

P = 128
J = 4
E = 512
Q = 512
N = 512
T = 1024
D = 128
H = 2
NH = N // H
NA = 128
NV = 320
QH = Q // 2


def tile_attend_bwd_kernel(tc, doT, vT, p, delta, qm, offs, out):
    nc = tc.nc
    with ExitStack() as ctx:
        keep = ctx.enter_context(tc.tile_pool(name="keep", bufs=1))
        psum = ctx.enter_context(tc.psum_pool(name="psum", bufs=1))

        offsets = keep.tile([P, N // 16], U16, name="offsets")

        v_rows = vT.rearrange("(p j) t -> p j t", j=J)
        v_raw = []
        for j in range(J):
            t = keep.tile([P, T], F32, name=f"v_raw{j}")
            nc.sync.dma_start(out=t[:], in_=v_rows[:, j, :])
            v_raw.append(t)
            if j == 0:
                nc.sync.dma_start(offsets[:], offs)

        do_rows = doT[0].rearrange("(p j) q -> p j q", j=J)
        do_raw = []
        for h in range(2):
            t = keep.tile([P, J, QH], F32, name=f"do_raw{h}")
            nc.sync.dma_start(out=t[:], in_=do_rows[:, :, h * QH : (h + 1) * QH])
            do_raw.append(t)

        p_rows = p[0].rearrange("(p j) s -> p j s", j=J)
        p_raw = {}
        for h in (1, 0):
            t = keep.tile([P, J, NH], F32, name=f"p_raw{h}")
            nc.sync.dma_start(out=t[:], in_=p_rows[:, :, h * NH : (h + 1) * NH])
            p_raw[h] = t
            if h == 1:
                qm_raw = keep.tile([P, J, D], F32, name="qm_raw")
                nc.sync.dma_start(out=qm_raw[:], in_=qm[0].rearrange("(p j) d -> p j d", j=J))

        delta_col = keep.tile([P, J], F32, name="delta_col")
        nc.scalar.dma_start(out=delta_col[:], in_=delta[0].rearrange("(p j) o -> p (j o)", j=J))
        minus_delta = keep.tile([P, J], F32, name="minus_delta")
        nc.gpsimd.tensor_scalar(minus_delta[:], delta_col[:], -1.0, None, ALU.mult)

        warm = keep.tile([P, 1], F32, name="warm")
        warm_out = keep.tile([P, 1], F32, name="warm_out")
        nc.gpsimd.memset(warm[:], 0.0)
        nc.scalar.activation(warm_out[:], warm[:], ACT.Identity)
        window = keep.tile([P, T], F32, name="window")
        nc.gpsimd.memset(window[:], 0.0)
        ds_codes = []
        ds_scales = []
        for h in range(2):
            c = keep.tile([P, N], U32, name=f"ds_codes{h}", align_bytes=64)
            s = keep.tile([P, N], U8, name=f"ds_scales{h}", align_bytes=64)
            fill = slice(NA, N) if h == 0 else slice(0, NA)
            nc.gpsimd.memset(c[:, fill], 0)
            nc.gpsimd.memset(s[:, fill].bitcast(U32), 0)
            ds_codes.append(c)
            ds_scales.append(s)

        identity = keep.tile([P, P], F32, name="identity")
        make_identity(nc, identity[:])
        spare = []
        for b in range(2):
            spare.append(psum.tile([P, 4, P], F32, name=f"spare{b}"))
        turns = [0]

        def keep_warm(src):
            b = turns[0] % 8
            turns[0] += 1
            nc.tensor.transpose(spare[b // 4][:, b % 4, :], src, identity[:])

        v_got = keep.tile([P, J, N], F32, name="v_got")
        v_cols = keep.tile([P, J * N], BF16, name="v_cols", align_bytes=64)

        def interleave_v(engine_copy, pair, s0, s1):
            js = slice(2 * pair, 2 * pair + 2)
            engine_copy(
                v_cols[:, J * s0 : J * s1].rearrange("p (c i j) -> p c j i", i=4, j=J)[:, :, js, :],
                v_got[:, js, s0:s1].rearrange("p j (c i) -> p c j i", i=4),
            )

        for j in range(J):
            nc.vector.tensor_copy(v_got[:, j, :], v_raw[j][:].indirect(offsets[:]))
            if j == 1:
                interleave_v(nc.scalar.copy, 0, 0, N)
        for b in range(10):
            keep_warm(v_raw[3][:, b % 8 * P : (b % 8 + 1) * P])
        for h, n in ((0, 8), (1, 6)):
            for b in range(n):
                keep_warm(do_raw[h][:, b // 2, b % 2 * P : (b % 2 + 1) * P])
        interleave_v(nc.vector.tensor_copy, 1, 0, NV)
        interleave_v(nc.scalar.copy, 1, NV, N)

        do_cols = keep.tile([P, J * Q], BF16, name="do_cols", align_bytes=64)
        do_view = do_cols[:].rearrange("p (t m j) -> p m j t", t=J, j=J)
        MH = QH // J
        v_codes = keep.tile([P, N], U32, name="v_codes", align_bytes=64)
        v_scales = keep.tile([P, N], U8, name="v_scales", align_bytes=64)
        nc.vector.quantize_mx(out=v_codes[:].bitcast(E4M3X4), scales=v_scales[:], in_=v_cols[:])
        for h, m0, m1 in ((0, 0, MH), (1, 0, MH // 2), (1, MH // 2, MH)):
            dst = do_view[:, h * MH + m0 : h * MH + m1, :, :]
            src = do_raw[h][:, :, m0 * J : m1 * J].rearrange("p j (m t) -> p m j t", t=J)
            if m0 == 0:
                nc.scalar.activation(dst, src, ACT.Copy)
            else:
                nc.vector.tensor_copy(dst, src)

        do_codes = keep.tile([P, Q], U32, name="do_codes", align_bytes=64)
        do_scales = keep.tile([P, Q], U8, name="do_scales", align_bytes=64)
        dp = []
        for t in range(J):
            cols = slice(t * P, (t + 1) * P)
            nc.vector.quantize_mx(
                out=do_codes[:, cols].bitcast(E5M2X4),
                scales=do_scales[:, cols],
                in_=do_cols[:, t * P * J : (t + 1) * P * J],
            )
            bank = psum.tile([P, N], F32, name=f"dp{t}")
            nc.tensor.matmul_mx(
                out=bank[:],
                lhsT=do_codes[:, cols].bitcast(E5M2X4),
                lhsT_scale=do_scales[:, cols],
                rhs=v_codes[:].bitcast(E4M3X4),
                rhs_scale=v_scales[:],
                start=True,
                stop=True,
            )
            dp.append(bank)

        qm_cols = keep.tile([P, J * D], BF16, name="qm_cols", align_bytes=64)
        nc.gpsimd.tensor_scalar(
            qm_cols[:].rearrange("p (c i j) -> p c j i", i=4, j=J),
            qm_raw[:].rearrange("p j (c i) -> p c j i", i=4),
            1.0,
            0.0,
            ALU.mult,
            ALU.add,
        )
        qm_codes = keep.tile([P, D], U32, name="qm_codes", align_bytes=64)
        qm_scales = keep.tile([P, D], U8, name="qm_scales", align_bytes=64)

        x = keep.tile([P, J, NH], F32, name="x")
        ds_rows = keep.tile([P, J, NH], BF16, name="ds_rows")
        for t in range(J):
            nc.scalar.activation(x[:, t, :], dp[t][:, 0:NH], ACT.Identity, bias=minus_delta[:, t : t + 1])
            nc.vector.scalar_tensor_tensor(
                ds_rows[:, t, :], dp[t][:, NH:N], delta_col[:, t : t + 1], p_raw[1][:, t, :], ALU.subtract, ALU.mult
            )
        for t in range(J):
            for b in range(NH // P):
                keep_warm(x[:, t, b * P : (b + 1) * P])
        for t in range(J):
            for b in range(NH // P):
                keep_warm(p_raw[0][:, t, b * P : (b + 1) * P])
        ds_tail = keep.tile([P, J * NH], BF16, name="ds_tail", align_bytes=64)
        nc.scalar.copy(
            ds_tail[:].rearrange("p (c i j) -> p c j i", i=4, j=J),
            ds_rows[:].rearrange("p j (c i) -> p c j i", i=4),
        )
        nc.vector.quantize_mx(out=qm_codes[:].bitcast(E4M3X4), scales=qm_scales[:], in_=qm_cols[:])
        ds_head = []
        for a in range(2):
            cols = slice(a * NA, (a + 1) * NA)
            d = keep.tile([P, J * NA], BF16, name=f"ds_head{a}", align_bytes=64)
            nc.vector.tensor_tensor(
                d[:].rearrange("p (c i j) -> p c j i", i=4, j=J),
                x[:, :, cols].rearrange("p j (c i) -> p c j i", i=4),
                p_raw[0][:, :, cols].rearrange("p j (c i) -> p c j i", i=4),
                ALU.mult,
            )
            ds_head.append(d)

        def quantise_ds(h, cols, src):
            nc.vector.quantize_mx(out=ds_codes[h][:, cols].bitcast(E5M2X4), scales=ds_scales[h][:, cols], in_=src)

        dk_cols = []

        def keys_gradient(h, cols):
            dk = psum.tile([P, N], F32, name=f"dk{h}")
            nc.tensor.matmul_mx(
                out=dk[:],
                lhsT=qm_codes[:].bitcast(E4M3X4),
                lhsT_scale=qm_scales[:],
                rhs=ds_codes[h][:].bitcast(E5M2X4),
                rhs_scale=ds_scales[h][:],
                start=True,
                stop=True,
            )
            for c0, c1 in cols:
                d = keep.tile([P, c1 - c0], F32, name=f"dk_cols{c0}")
                nc.scalar.activation(d[:], dk[:, c0:c1], ACT.Copy)
                dk_cols.append((c0, c1, d))

        quantise_ds(0, slice(0, NA), ds_head[0][:])
        keys_gradient(0, ((0, NA),))
        quantise_ds(1, slice(NA, NH), ds_head[1][:])
        quantise_ds(1, slice(NH, N), ds_tail[:])
        keys_gradient(1, ((NA, N),))
        for c0, c1, d in dk_cols:
            nc.vector.tensor_copy(window[:].indirect(offsets[:, c0 // 16 : c1 // 16]), d[:])
        nc.sync.dma_start(out=out, in_=window[:])
